import numpy as np, ml_dtypes
CORES = [12,28,60,100,156,228]
N = 6
GR, GC, TK = 3, 2, 128
RA = [[-1,-2,2],[-2,1,-2],[2,-2,1]]
CB = [[-2,1],[-2,-1]]
def setup_inputs(rng):
    return {"x": rng.standard_normal((N, 128, TK), dtype=np.float32).astype(ml_dtypes.bfloat16), "a": (rng.standard_normal((N, 128, 128), dtype=np.float32) / 11).astype(ml_dtypes.bfloat16)}
def setup_inputs_big(rng):
    d = setup_inputs(rng)
    for k in ("x", "a"): d[k] = (d[k].astype(np.float32) * 1024.0).astype(d[k].dtype)
    return d
def setup_inputs_small(rng):
    d = setup_inputs(rng)
    for k in ("x", "a"): d[k] = (d[k].astype(np.float32) * (1 / 1024.0)).astype(d[k].dtype)
    return d
def setup_inputs_apart(rng):
    d = setup_inputs(rng)
    f = (10.0 ** rng.permutation(np.linspace(-1.5, 1.5, N))).astype(np.float32).reshape(N, 1, 1)
    for k in ("x", "a"): d[k] = (d[k].astype(np.float32) * f).astype(d[k].dtype)
    return d
def reference(x, a):
    X, A = x.astype(np.float64), a.astype(np.float64)
    y = np.zeros((N, 128, TK))
    for i in range(GR):
        for j in range(GC):
            t = sum(RA[i][k] * CB[j][l] * X[k * GC + l] for k in range(GR) for l in range(GC))
            y[i * GC + j] = A[i * GC + j].T @ t
    return {"y": y.astype(ml_dtypes.bfloat16)}

@@ -1,0 +1,131 @@
+from concourse.bass import DstId, RemoteDMATransfer
+from concourse.mybir import AluOpType
+
+NR = 6
+W = 128
+DIRECT = 2
+
+SCRATCH = {
+    "xd": ("dram", [128, W], "bfloat16"),
+    "hx": ("dram", [128, W], "bfloat16"),
+    "xs": ("sbuf", [128, NR * W], "bfloat16"),
+    "a0": ("sbuf", [128, W], "bfloat16"),
+    "cb": ("sbuf", [128, NR * W], "bfloat16"),
+    "asc": ("sbuf", [128, NR * W], "bfloat16"),
+    "yb": ("sbuf", [128, W], "bfloat16"),
+    "ps": ("psum", [128, W], "float32"),
+}
+SEMAPHORES = ["ld", "lx", "la", "vs", "va", "mm", "cp", "st", "sent", "hin"] + ["arr%d" % s for s in range(NR)]
+
+
+def _count(mask):
+    return sum((mask >> b) & 1 for b in range(mask.bit_length()))
+
+
+def _chipmates(topo, c):
+    k = topo.CORES_PER_CHIP
+    return [h for h in range(max(0, c - k + 1), c + k)
+            if h != c and topo.host(h) == topo.host(c) and topo.chip(h) == topo.chip(c)]
+
+
+def _routes(cores, topo):
+    n = len(cores)
+    group = {s: [d for d in range(n) if d == s or topo.may_write(cores[s], cores[d])] for s in range(n)}
+    routes = {}
+    for s in range(n):
+        c = cores[s]
+        order = [(s + t) % n for t in range(1, n)]
+        near = [d for d in order if d in group[s]]
+        far = [d for d in order if d not in group[s]]
+        free = [h for h in _chipmates(topo, c) if h not in cores]
+        for d in near[:DIRECT]:
+            routes[(s, d)] = None
+        for d in far:
+            other = (group[s].index(s) + group[d].index(d)) % 2
+            cand = sorted([h for h in free if topo.may_write(h, cores[d])],
+                          key=lambda h: int(topo.die(h) != topo.die(c)) != other)
+            routes[(s, d)] = cand[0]
+            free.remove(cand[0])
+        for d in near[DIRECT:]:
+            cand = sorted([h for h in free if topo.may_write(h, cores[d])],
+                          key=lambda h: (topo.die(h) == topo.die(c), any(topo.may_write(h, cores[f]) for f in far)))
+            routes[(s, d)] = cand[0]
+            free.remove(cand[0])
+    return routes
+
+
+def _slot(buf, k):
+    return buf[:, k * W:(k + 1) * W]
+
+
+def _dst(topo, d, src):
+    rid, pid = topo.addr(d, src)
+    return DstId(rid=rid, pnc=pid)
+
+
+def rank_program(g, core, T, topo):
+    cores = list(T.cores)
+    routes = _routes(cores, topo)
+    rank = T.rank_of(core)
+
+    if rank is None:
+        jobs = [sd for sd, h in routes.items() if h == core]
+        if not jobs:
+            return
+        s, d = jobs[0]
+        m_in = topo.mask(cores[s], core) & ~topo.mask(core, cores[d])
+        m_out = topo.mask(core, cores[d])
+        rid, pid = topo.addr(cores[d], core)
+        g.wait_ge(T.sem.hin, _count(m_in))
+        g.remote_dma(_slot(T.xs, s), T.hx[:], T.sem["arr%d" % s], T.sem.sent, pid, rid, m_out)
+        g.wait_ge(T.sem.sent, _count(m_out))
+        return
+
+    i, j = rank // 2, rank % 2
+    RA, CB = T.tables["RA"], T.tables["CB"]
+    coef = [RA[i][s // 2] * CB[j][s % 2] for s in range(NR)]
+    scaled = sorted(set(c for c in coef if c != 1))
+
+    g.sync.dma_start(T.xd[:], T.x[:]).then_inc(T.sem.ld, 16)
+    g.scalar.dma_start(T.a0[:], T.a[:]).then_inc(T.sem.la, 16)
+    g.scalar.dma_start(_slot(T.xs, rank), T.x[:]).then_inc(T.sem.lx, 16)
+
+    for k, c in enumerate(scaled):
+        g.vector.memset(_slot(T.cb, k), float(c)).then_inc(T.sem.vs, 1)
+    g.vector.wait_ge(T.sem.vs, len(scaled))
+    g.vector.wait_ge(T.sem.la, 16)
+    for k, c in enumerate(scaled):
+        g.vector.tensor_tensor(_slot(T.asc, k), T.a0[:], _slot(T.cb, k), AluOpType.mult).then_inc(T.sem.va, 1)
+
+    helpers = [routes[(rank, d)] for d in range(NR) if d != rank and routes[(rank, d)] is not None]
+    direct = [d for d in range(NR) if d != rank and routes[(rank, d)] is None]
+    m_off = topo.mask(core, cores[direct[0]])
+    m_on = topo.mask(core, helpers[0]) & ~m_off
+    g.wait_ge(T.sem.ld, 16)
+    g.remote_dma_fused([RemoteDMATransfer(
+        dst_ids=[_dst(topo, h, core) for h in helpers], dma_engine_mask=m_on, remote_sem=T.sem.hin,
+        srcs=[T.xd[:]], dsts=[T.hx[:] for h in helpers], alu_op=0)], local_sem=T.sem.sent)
+    g.remote_dma_fused([RemoteDMATransfer(
+        dst_ids=[_dst(topo, cores[d], core) for d in direct], dma_engine_mask=m_off, remote_sem=T.sem["arr%d" % rank],
+        srcs=[T.xd[:]], dsts=[_slot(T.xs, rank) for d in direct], alu_op=0)], local_sem=T.sem.sent)
+
+    order = [rank] + [s for s in range(NR) if s != rank and routes[(s, rank)] is None] \
+                   + [s for s in range(NR) if s != rank and routes[(s, rank)] is not None]
+    g.tensor.wait_ge(T.sem.la, 16)
+    g.tensor.wait_ge(T.sem.va, len(scaled))
+    for n, s in enumerate(order):
+        if s == rank:
+            g.tensor.wait_ge(T.sem.lx, 16)
+        else:
+            src = cores[s] if routes[(s, rank)] is None else routes[(s, rank)]
+            g.tensor.wait_ge(T.sem["arr%d" % s], _count(topo.mask(src, core)))
+        lhsT = T.a0[:] if coef[s] == 1 else _slot(T.asc, scaled.index(coef[s]))
+        mm = g.tensor.matmul(T.ps[:], lhsT, _slot(T.xs, s), n == 0, n == NR - 1)
+    mm.then_inc(T.sem.mm, 1)
+
+    g.vector.wait_ge(T.sem.mm, 1)
+    g.vector.tensor_copy(T.yb[:], T.ps[:]).then_inc(T.sem.cp, 1)
+    g.sync.wait_ge(T.sem.cp, 1)
+    g.sync.dma_start(T.y[:], T.yb[:]).then_inc(T.sem.st, 16)
+    g.sync.wait_ge(T.sem.st, 16)
+    g.wait_ge(T.sem.sent, _count(m_on) + _count(m_off))

@@ -3,19 +3,24 @@ from concourse.mybir import AluOpType
 
 NR = 6
 W = 128
-DIRECT = 2
+NW = 2
+HW = W // 2
 
 SCRATCH = {
-    "xd": ("dram", [128, W], "bfloat16"),
-    "hx": ("dram", [128, W], "bfloat16"),
+    "xn": ("dram", [128, NW], "bfloat16"),
+    "xw": ("dram", [128, W - NW], "bfloat16"),
+    "hn": ("dram", [128, NW], "bfloat16"),
+    "hw": ("dram", [128, W - NW], "bfloat16"),
     "xs": ("sbuf", [128, NR * W], "bfloat16"),
     "a0": ("sbuf", [128, W], "bfloat16"),
     "cb": ("sbuf", [128, NR * W], "bfloat16"),
     "asc": ("sbuf", [128, NR * W], "bfloat16"),
     "yb": ("sbuf", [128, W], "bfloat16"),
-    "ps": ("psum", [128, W], "float32"),
+    "ps0": ("psum", [128, 512], "float32"),
+    "ps1": ("psum", [128, 512], "float32"),
 }
-SEMAPHORES = ["ld", "lx", "la", "vs", "va", "mm", "cp", "st", "sent", "hin"] + ["arr%d" % s for s in range(NR)]
+SEMAPHORES = ["ldn", "ldw", "lx", "la", "vs", "va", "mm0", "mm1", "cp", "st", "sent", "hinn", "hinw"] \
+    + ["arr%d" % s for s in range(NR)]
 
 
 def _count(mask):
@@ -28,30 +33,28 @@ def _chipmates(topo, c):
             if h != c and topo.host(h) == topo.host(c) and topo.chip(h) == topo.chip(c)]
 
 
-def _routes(cores, topo):
+def _plan(cores, topo):
     n = len(cores)
     group = {s: [d for d in range(n) if d == s or topo.may_write(cores[s], cores[d])] for s in range(n)}
-    routes = {}
+    near, far = {}, {}
     for s in range(n):
         c = cores[s]
-        order = [(s + t) % n for t in range(1, n)]
-        near = [d for d in order if d in group[s]]
-        far = [d for d in order if d not in group[s]]
+        own = group[s]
+        a = own.index(s)
+        near[s] = [own[(a + t) % len(own)] for t in range(1, len(own))]
+        rest = [d for d in range(n) if d not in own]
+        rest = [rest[(t + a // 2) % len(rest)] for t in range(len(rest))]
+        if a % 2:
+            rest.reverse()
         free = [h for h in _chipmates(topo, c) if h not in cores]
-        for d in near[:DIRECT]:
-            routes[(s, d)] = None
-        for d in far:
-            other = (group[s].index(s) + group[d].index(d)) % 2
+        far[s] = []
+        for d in rest:
+            other = (a + group[d].index(d)) % 2
             cand = sorted([h for h in free if topo.may_write(h, cores[d])],
                           key=lambda h: int(topo.die(h) != topo.die(c)) != other)
-            routes[(s, d)] = cand[0]
+            far[s].append((d, cand[0]))
             free.remove(cand[0])
-        for d in near[DIRECT:]:
-            cand = sorted([h for h in free if topo.may_write(h, cores[d])],
-                          key=lambda h: (topo.die(h) == topo.die(c), any(topo.may_write(h, cores[f]) for f in far)))
-            routes[(s, d)] = cand[0]
-            free.remove(cand[0])
-    return routes
+    return near, far
 
 
 def _slot(buf, k):
@@ -65,20 +68,23 @@ def _dst(topo, d, src):
 
 def rank_program(g, core, T, topo):
     cores = list(T.cores)
-    routes = _routes(cores, topo)
+    near, far = _plan(cores, topo)
     rank = T.rank_of(core)
+    m_rank = {s: topo.mask(cores[s], cores[near[s][0]]) for s in range(NR)}
+    m_one = {s: m_rank[s] & -m_rank[s] for s in range(NR)}
 
     if rank is None:
-        jobs = [sd for sd, h in routes.items() if h == core]
+        jobs = [(s, d) for s in range(NR) for d, h in far[s] if h == core]
         if not jobs:
             return
         s, d = jobs[0]
-        m_in = topo.mask(cores[s], core) & ~topo.mask(core, cores[d])
         m_out = topo.mask(core, cores[d])
         rid, pid = topo.addr(cores[d], core)
-        g.wait_ge(T.sem.hin, _count(m_in))
-        g.remote_dma(_slot(T.xs, s), T.hx[:], T.sem["arr%d" % s], T.sem.sent, pid, rid, m_out)
-        g.wait_ge(T.sem.sent, _count(m_out))
+        g.wait_ge(T.sem.hinn, _count(m_one[s]))
+        g.remote_dma(T.xs[:, s * W:s * W + NW], T.hn[:], T.sem["arr%d" % s], T.sem.sent, pid, rid, m_out)
+        g.wait_ge(T.sem.hinw, _count(m_rank[s]))
+        g.remote_dma(T.xs[:, s * W + NW:(s + 1) * W], T.hw[:], T.sem["arr%d" % s], T.sem.sent, pid, rid, m_out)
+        g.wait_ge(T.sem.sent, 2 * _count(m_out))
         return
 
     i, j = rank // 2, rank % 2
@@ -86,9 +92,11 @@ def rank_program(g, core, T, topo):
     coef = [RA[i][s // 2] * CB[j][s % 2] for s in range(NR)]
     scaled = sorted(set(c for c in coef if c != 1))
 
-    g.sync.dma_start(T.xd[:], T.x[:]).then_inc(T.sem.ld, 16)
-    g.scalar.dma_start(T.a0[:], T.a[:]).then_inc(T.sem.la, 16)
+    g.sync.dma_start(T.xn[:], T.x[:, 0:NW]).then_inc(T.sem.ldn, 16)
+    g.sync.dma_start(T.xw[:], T.x[:, NW:W]).then_inc(T.sem.ldw, 16)
+    g.scalar.wait_ge(T.sem.ldn, 16)
     g.scalar.dma_start(_slot(T.xs, rank), T.x[:]).then_inc(T.sem.lx, 16)
+    g.scalar.dma_start(T.a0[:], T.a[:]).then_inc(T.sem.la, 16)
 
     for k, c in enumerate(scaled):
         g.vector.memset(_slot(T.cb, k), float(c)).then_inc(T.sem.vs, 1)
@@ -97,35 +105,46 @@ def rank_program(g, core, T, topo):
     for k, c in enumerate(scaled):
         g.vector.tensor_tensor(_slot(T.asc, k), T.a0[:], _slot(T.cb, k), AluOpType.mult).then_inc(T.sem.va, 1)
 
-    helpers = [routes[(rank, d)] for d in range(NR) if d != rank and routes[(rank, d)] is not None]
-    direct = [d for d in range(NR) if d != rank and routes[(rank, d)] is None]
-    m_off = topo.mask(core, cores[direct[0]])
-    m_on = topo.mask(core, helpers[0]) & ~m_off
-    g.wait_ge(T.sem.ld, 16)
+    helpers = [h for d, h in far[rank]]
+    g.wait_ge(T.sem.ldn, 16)
     g.remote_dma_fused([RemoteDMATransfer(
-        dst_ids=[_dst(topo, h, core) for h in helpers], dma_engine_mask=m_on, remote_sem=T.sem.hin,
-        srcs=[T.xd[:]], dsts=[T.hx[:] for h in helpers], alu_op=0)], local_sem=T.sem.sent)
+        dst_ids=[_dst(topo, h, core) for h in helpers], dma_engine_mask=m_one[rank], remote_sem=T.sem.hinn,
+        srcs=[T.xn[:]], dsts=[T.hn[:] for h in helpers], alu_op=0)], local_sem=T.sem.sent)
+    g.wait_ge(T.sem.ldw, 16)
     g.remote_dma_fused([RemoteDMATransfer(
-        dst_ids=[_dst(topo, cores[d], core) for d in direct], dma_engine_mask=m_off, remote_sem=T.sem["arr%d" % rank],
-        srcs=[T.xd[:]], dsts=[_slot(T.xs, rank) for d in direct], alu_op=0)], local_sem=T.sem.sent)
+        dst_ids=[_dst(topo, h, core) for h in helpers], dma_engine_mask=m_rank[rank], remote_sem=T.sem.hinw,
+        srcs=[T.xw[:]], dsts=[T.hw[:] for h in helpers], alu_op=0)], local_sem=T.sem.sent)
+    g.wait_ge(T.sem.lx, 16)
+    g.remote_dma_fused([RemoteDMATransfer(
+        dst_ids=[_dst(topo, cores[d], core) for d in near[rank]], dma_engine_mask=m_rank[rank],
+        remote_sem=T.sem["arr%d" % rank],
+        srcs=[_slot(T.xs, rank)], dsts=[_slot(T.xs, rank) for d in near[rank]], alu_op=0)], local_sem=T.sem.sent)
 
-    order = [rank] + [s for s in range(NR) if s != rank and routes[(s, rank)] is None] \
-                   + [s for s in range(NR) if s != rank and routes[(s, rank)] is not None]
+    direct = sorted([s for s in range(NR) if rank in near[s]], key=lambda s: near[s].index(rank))
+    cross = sorted([s for s in range(NR) if rank in [d for d, h in far[s]]],
+                   key=lambda s: [d for d, h in far[s]].index(rank))
+    order = [rank] + direct + cross
+    ps = [T.ps0, T.ps1]
     g.tensor.wait_ge(T.sem.la, 16)
     g.tensor.wait_ge(T.sem.va, len(scaled))
     for n, s in enumerate(order):
         if s == rank:
             g.tensor.wait_ge(T.sem.lx, 16)
+        elif s in direct:
+            g.tensor.wait_ge(T.sem["arr%d" % s], _count(m_rank[s]))
         else:
-            src = cores[s] if routes[(s, rank)] is None else routes[(s, rank)]
-            g.tensor.wait_ge(T.sem["arr%d" % s], _count(topo.mask(src, core)))
+            h = [hh for d, hh in far[s] if d == rank][0]
+            g.tensor.wait_ge(T.sem["arr%d" % s], 2 * _count(topo.mask(h, core)))
         lhsT = T.a0[:] if coef[s] == 1 else _slot(T.asc, scaled.index(coef[s]))
-        mm = g.tensor.matmul(T.ps[:], lhsT, _slot(T.xs, s), n == 0, n == NR - 1)
-    mm.then_inc(T.sem.mm, 1)
+        for b in range(2):
+            mm = g.tensor.matmul(ps[b][:, 0:HW], lhsT, T.xs[:, s * W + b * HW:s * W + (b + 1) * HW], n == 0, n == NR - 1)
+            if n == NR - 1:
+                mm.then_inc(T.sem["mm%d" % b], 1)
 
-    g.vector.wait_ge(T.sem.mm, 1)
-    g.vector.tensor_copy(T.yb[:], T.ps[:]).then_inc(T.sem.cp, 1)
-    g.sync.wait_ge(T.sem.cp, 1)
+    for b in range(2):
+        g.vector.wait_ge(T.sem["mm%d" % b], 1)
+        g.vector.tensor_copy(T.yb[:, b * HW:(b + 1) * HW], ps[b][:, 0:HW]).then_inc(T.sem.cp, 1)
+    g.sync.wait_ge(T.sem.cp, 2)
     g.sync.dma_start(T.y[:], T.yb[:]).then_inc(T.sem.st, 16)
     g.sync.wait_ge(T.sem.st, 16)
-    g.wait_ge(T.sem.sent, _count(m_on) + _count(m_off))
+    g.wait_ge(T.sem.sent, _count(m_one[rank]) + 2 * _count(m_rank[rank]))

from concourse.bass import DstId, RemoteDMATransfer
from concourse.mybir import AluOpType

NR = 6
W = 128
NW = 2
HW = W // 2

SCRATCH = {
    "xn": ("dram", [128, NW], "bfloat16"),
    "xw": ("dram", [128, W - NW], "bfloat16"),
    "hn": ("dram", [128, NW], "bfloat16"),
    "hw": ("dram", [128, W - NW], "bfloat16"),
    "xs": ("sbuf", [128, NR * W], "bfloat16"),
    "a0": ("sbuf", [128, W], "bfloat16"),
    "cb": ("sbuf", [128, NR * W], "bfloat16"),
    "asc": ("sbuf", [128, NR * W], "bfloat16"),
    "yb": ("sbuf", [128, W], "bfloat16"),
    "ps0": ("psum", [128, 512], "float32"),
    "ps1": ("psum", [128, 512], "float32"),
}
SEMAPHORES = ["ldn", "ldw", "lx", "la", "vs", "va", "mm0", "mm1", "cp", "st", "sent", "hinn", "hinw"] \
    + ["arr%d" % s for s in range(NR)]


def _count(mask):
    return sum((mask >> b) & 1 for b in range(mask.bit_length()))


def _chipmates(topo, c):
    k = topo.CORES_PER_CHIP
    return [h for h in range(max(0, c - k + 1), c + k)
            if h != c and topo.host(h) == topo.host(c) and topo.chip(h) == topo.chip(c)]


def _plan(cores, topo):
    n = len(cores)
    group = {s: [d for d in range(n) if d == s or topo.may_write(cores[s], cores[d])] for s in range(n)}
    near, far = {}, {}
    for s in range(n):
        c = cores[s]
        own = group[s]
        a = own.index(s)
        near[s] = [own[(a + t) % len(own)] for t in range(1, len(own))]
        rest = [d for d in range(n) if d not in own]
        rest = [rest[(t + a // 2) % len(rest)] for t in range(len(rest))]
        if a % 2:
            rest.reverse()
        free = [h for h in _chipmates(topo, c) if h not in cores]
        far[s] = []
        for d in rest:
            other = (a + group[d].index(d)) % 2
            cand = sorted([h for h in free if topo.may_write(h, cores[d])],
                          key=lambda h: int(topo.die(h) != topo.die(c)) != other)
            far[s].append((d, cand[0]))
            free.remove(cand[0])
    return near, far


def _slot(buf, k):
    return buf[:, k * W:(k + 1) * W]


def _dst(topo, d, src):
    rid, pid = topo.addr(d, src)
    return DstId(rid=rid, pnc=pid)


def rank_program(g, core, T, topo):
    cores = list(T.cores)
    near, far = _plan(cores, topo)
    rank = T.rank_of(core)
    m_rank = {s: topo.mask(cores[s], cores[near[s][0]]) for s in range(NR)}
    m_one = {s: m_rank[s] & -m_rank[s] for s in range(NR)}

    if rank is None:
        jobs = [(s, d) for s in range(NR) for d, h in far[s] if h == core]
        if not jobs:
            return
        s, d = jobs[0]
        m_out = topo.mask(core, cores[d])
        rid, pid = topo.addr(cores[d], core)
        g.wait_ge(T.sem.hinn, _count(m_one[s]))
        g.remote_dma(T.xs[:, s * W:s * W + NW], T.hn[:], T.sem["arr%d" % s], T.sem.sent, pid, rid, m_out)
        g.wait_ge(T.sem.hinw, _count(m_rank[s]))
        g.remote_dma(T.xs[:, s * W + NW:(s + 1) * W], T.hw[:], T.sem["arr%d" % s], T.sem.sent, pid, rid, m_out)
        g.wait_ge(T.sem.sent, 2 * _count(m_out))
        return

    i, j = rank // 2, rank % 2
    RA, CB = T.tables["RA"], T.tables["CB"]
    coef = [RA[i][s // 2] * CB[j][s % 2] for s in range(NR)]
    scaled = sorted(set(c for c in coef if c != 1))

    g.sync.dma_start(T.xn[:], T.x[:, 0:NW]).then_inc(T.sem.ldn, 16)
    g.sync.dma_start(T.xw[:], T.x[:, NW:W]).then_inc(T.sem.ldw, 16)
    g.scalar.wait_ge(T.sem.ldn, 16)
    g.scalar.dma_start(_slot(T.xs, rank), T.x[:]).then_inc(T.sem.lx, 16)
    g.scalar.dma_start(T.a0[:], T.a[:]).then_inc(T.sem.la, 16)

    for k, c in enumerate(scaled):
        g.vector.memset(_slot(T.cb, k), float(c)).then_inc(T.sem.vs, 1)
    g.vector.wait_ge(T.sem.vs, len(scaled))
    g.vector.wait_ge(T.sem.la, 16)
    for k, c in enumerate(scaled):
        g.vector.tensor_tensor(_slot(T.asc, k), T.a0[:], _slot(T.cb, k), AluOpType.mult).then_inc(T.sem.va, 1)

    helpers = [h for d, h in far[rank]]
    g.wait_ge(T.sem.ldn, 16)
    g.remote_dma_fused([RemoteDMATransfer(
        dst_ids=[_dst(topo, h, core) for h in helpers], dma_engine_mask=m_one[rank], remote_sem=T.sem.hinn,
        srcs=[T.xn[:]], dsts=[T.hn[:] for h in helpers], alu_op=0)], local_sem=T.sem.sent)
    g.wait_ge(T.sem.ldw, 16)
    g.remote_dma_fused([RemoteDMATransfer(
        dst_ids=[_dst(topo, h, core) for h in helpers], dma_engine_mask=m_rank[rank], remote_sem=T.sem.hinw,
        srcs=[T.xw[:]], dsts=[T.hw[:] for h in helpers], alu_op=0)], local_sem=T.sem.sent)
    g.wait_ge(T.sem.lx, 16)
    g.remote_dma_fused([RemoteDMATransfer(
        dst_ids=[_dst(topo, cores[d], core) for d in near[rank]], dma_engine_mask=m_rank[rank],
        remote_sem=T.sem["arr%d" % rank],
        srcs=[_slot(T.xs, rank)], dsts=[_slot(T.xs, rank) for d in near[rank]], alu_op=0)], local_sem=T.sem.sent)

    direct = sorted([s for s in range(NR) if rank in near[s]], key=lambda s: near[s].index(rank))
    cross = sorted([s for s in range(NR) if rank in [d for d, h in far[s]]],
                   key=lambda s: [d for d, h in far[s]].index(rank))
    order = [rank] + direct + cross
    ps = [T.ps0, T.ps1]
    g.tensor.wait_ge(T.sem.la, 16)
    g.tensor.wait_ge(T.sem.va, len(scaled))
    for n, s in enumerate(order):
        if s == rank:
            g.tensor.wait_ge(T.sem.lx, 16)
        elif s in direct:
            g.tensor.wait_ge(T.sem["arr%d" % s], _count(m_rank[s]))
        else:
            h = [hh for d, hh in far[s] if d == rank][0]
            g.tensor.wait_ge(T.sem["arr%d" % s], 2 * _count(topo.mask(h, core)))
        lhsT = T.a0[:] if coef[s] == 1 else _slot(T.asc, scaled.index(coef[s]))
        for b in range(2):
            mm = g.tensor.matmul(ps[b][:, 0:HW], lhsT, T.xs[:, s * W + b * HW:s * W + (b + 1) * HW], n == 0, n == NR - 1)
            if n == NR - 1:
                mm.then_inc(T.sem["mm%d" % b], 1)

    for b in range(2):
        g.vector.wait_ge(T.sem["mm%d" % b], 1)
        g.vector.tensor_copy(T.yb[:, b * HW:(b + 1) * HW], ps[b][:, 0:HW]).then_inc(T.sem.cp, 1)
    g.sync.wait_ge(T.sem.cp, 2)
    g.sync.dma_start(T.y[:], T.yb[:]).then_inc(T.sem.st, 16)
    g.sync.wait_ge(T.sem.st, 16)
    g.wait_ge(T.sem.sent, _count(m_one[rank]) + 2 * _count(m_rank[rank]))
